import numpy as np
import ml_dtypes


def mxq(x, axis, fmt="e4m3"):
    dtype, down = {"e4m3": (ml_dtypes.float8_e4m3fn, 7), "e5m2": (ml_dtypes.float8_e5m2, 14)}[fmt]
    v = np.moveaxis(np.asarray(x, np.float32).astype(ml_dtypes.bfloat16).astype(np.float64), axis, -1)
    blocks = v.reshape(v.shape[:-1] + (-1, 32))
    amax = np.abs(blocks).max(-1, keepdims=True)
    byte = np.maximum(np.where(amax > 0, np.frexp(amax)[1] - 1 + 127, 0) - down, 1)
    scale = np.exp2(byte - 127.0)
    codes = (blocks / scale).astype(np.float32).astype(dtype).astype(np.float64)
    return np.moveaxis((codes * scale).reshape(v.shape), -1, axis)


WIDE = False


def mx_kscale(k):
    if not WIDE:
        return np.ones(k)
    levels = np.array([10, -10, 5, -5, 0])
    if k % 512:
        return np.exp2(np.random.permutation(np.resize(levels, k // 32))).repeat(32)
    a = np.empty((k // 512, 16))
    for p in range(k // 512):
        a[p, :8] = np.random.permutation(np.resize(levels, 8))
        for g in range(8):
            far = levels[np.abs(levels - a[p, g]) >= 10]
            a[p, g + 8] = far[np.random.randint(len(far))]
    return np.exp2(a.ravel()).repeat(32)


def f64(x):
    return np.asarray(x).astype(np.float64)


def striped(idx):
    return np.tile(idx.reshape(-1, 16).T, (8, 1)).astype(np.uint16)


def unstriped(offs):
    return offs[:16].T.reshape(-1).astype(np.int64)


def striped8(idx):
    return np.concatenate([x.reshape(-1, 16).T for x in idx]).astype(np.uint16)


def runs(offs, k):
    lists = np.stack([offs[16 * r : 16 * r + 16].T.reshape(-1) for r in range(8)]).astype(np.int64)
    return lists[np.arange(k) % 512 // 64]


def pack_weight(w):
    k, n = w.shape
    w = f64(np.asarray(w, np.float32).astype(ml_dtypes.bfloat16)).reshape(k // 32, 32, n)
    amax = np.abs(w).max(1)
    byte = np.clip(np.where(amax > 0, np.frexp(amax)[1] - 1 + 127 - 7, 1), 1, 254)
    scaled = (w * np.exp2(127.0 - byte)[:, None, :]).reshape(k, n).astype(np.float32)
    words = np.ascontiguousarray(scaled.reshape(k // 512, 128, 4, n).transpose(0, 1, 3, 2)).astype(ml_dtypes.float8_e4m3fn).view(np.uint8)
    return words, np.ascontiguousarray(byte.astype(np.uint8).reshape(k // 512, 16, n))


def unpack_weight(words, scales):
    g, p, n, _ = words.shape
    vals = np.ascontiguousarray(words).view(ml_dtypes.float8_e4m3fn).astype(np.float64) * np.repeat(np.exp2(scales.astype(np.float64) - 127.0), 8, axis=1)[..., None]
    return vals.transpose(0, 1, 3, 2).reshape(g * 512, n)


def gelu(v):
    return 0.5 * v * (1.0 + np.tanh(np.sqrt(2.0 / np.pi) * (v + 0.044715 * v**3)))


K, T, S, V, N, U, H = 512, 2048, 512, 512, 512, 1024, 512
P = 2 ** 7


def setup_inputs():
    n = np.random.standard_normal
    s = mx_kscale(K)[:, None]
    u = mx_kscale(H)
    packed_xT = pack_weight(n((K, T)) * s)
    return {
        "x_words": packed_xT[0],
        "x_scales": packed_xT[1],
        "w1": (n((K, H)) / np.sqrt(K) / s * u).astype(np.float32),
        "w2": (n((H, N)) / np.sqrt(H) / u[:, None]).astype(np.float32),
        "g1": np.tile(np.random.uniform(0.2, 1.0, V), (P, 1)).astype(np.float32),
        "g2": np.tile(np.random.uniform(0.2, 1.0, V), (P, 1)).astype(np.float32),
        "offs": striped(np.random.permutation(T)[:S]),
        "slot": striped8(np.stack([np.random.permutation(U)[:S] for _ in range(8)])),
        "c1": striped8(np.stack([np.random.permutation(U)[:V] for _ in range(8)])),
        "c2": striped8(np.stack([np.random.permutation(U)[:V] for _ in range(8)])),
    }


def reference(x_words, x_scales, w1, w2, g1, g2, offs, slot, c1, c2):
    xq = unpack_weight(x_words, x_scales)[:, unstriped(offs)]
    y = mxq(f64(w1), 0, "e4m3").T @ xq
    d = np.zeros((H, U))
    d[np.arange(H)[:, None], runs(slot, H)] = y
    z = gelu(d)
    h = mxq(f64(w2), 0, "e4m3").T @ mxq(z, 0, "e4m3")
    return (h[np.arange(N)[:, None], runs(c1, N)]) * f64(g1)[:1] + (h[np.arange(N)[:, None], runs(c2, N)]) * f64(g2)[:1]

@@ -1,0 +1,159 @@
+from contextlib import ExitStack
+
+import concourse.mybir as mybir
+
+K, T, S, V, N, U, H = 512, 2048, 512, 512, 512, 1024, 512
+FLOPS = 2 * K * H * S + 2 * H * N * U
+
+F32 = mybir.dt.float32
+BF16 = mybir.dt.bfloat16
+I32 = mybir.dt.int32
+U32 = mybir.dt.uint32
+U16 = mybir.dt.uint16
+U8 = mybir.dt.uint8
+FP8X4 = mybir.dt.float8_e4m3fn_x4
+MULT = mybir.AluOpType.mult
+ADD = mybir.AluOpType.add
+GELU = mybir.ActivationFunctionType.Gelu_apprx_tanh
+
+P = 128
+PACK = 4
+BANK = 512
+
+
+def tile_picked_dcomb_gelu_p_kernel(
+    tc, x_words, x_scales, w1, w2, g1, g2, offs, slot, c1, c2, out
+):
+    nc = tc.nc
+    with ExitStack() as ctx:
+        keep = ctx.enter_context(tc.tile_pool(name="keep", bufs=1))
+        psum = ctx.enter_context(tc.psum_pool(name="psum", bufs=8))
+
+        def load_list(src, name):
+            tile = keep.tile([P, S // 16], U16, name=name)
+            nc.sync.dma_start(tile[:], src)
+            return tile
+
+        def load_weight(src, name):
+            raw = keep.tile([P, PACK, BANK], F32, name=name)
+            nc.sync.dma_start(out=raw[:], in_=src.rearrange("(p j) c -> p j c", j=PACK))
+            return raw
+
+        def deal_views(raw, grouped):
+            return (
+                grouped[:].rearrange("p (t m j) -> p m t j", t=PACK, j=PACK),
+                raw[:].rearrange("p j (m t) -> p m t j", t=PACK),
+            )
+
+        xs_all = keep.tile([P, T], U8, name="xs_all", align_bytes=64)
+        nc.vector.memset(xs_all[:].bitcast(I32), 0)
+        offs_t = load_list(offs, "offs_t")
+        for q in range(4):
+            nc.sync.dma_start(
+                out=xs_all[32 * q : 32 * q + 4, :].bitcast(I32),
+                in_=x_scales[0, 4 * q : 4 * q + 4, :].bitcast(I32),
+            )
+        w1_raw = load_weight(w1, "w1_raw")
+        xw_all = keep.tile([P, T], I32, name="xw_all", align_bytes=64)
+        nc.sync.dma_start(out=xw_all[:], in_=x_words[0].rearrange("p c r -> p (c r)").bitcast(I32))
+        slot_t = load_list(slot, "slot_t")
+        w2_raw = load_weight(w2, "w2_raw")
+        c1_t = load_list(c1, "c1_t")
+        c2_t = load_list(c2, "c2_t")
+        g1_t = keep.tile([P, V], F32, name="g1_t")
+        nc.sync.dma_start(out=g1_t[:], in_=g1)
+        g2_t = keep.tile([P, V], F32, name="g2_t")
+        nc.sync.dma_start(out=g2_t[:], in_=g2)
+
+        win = {}
+        for t in (1, 3, 0, 2):
+            width = U if t % 2 else 2 * U
+            win[t] = keep.tile([P, width], F32, name=f"win{t}")
+            nc.vector.memset(win[t][:, 0:U], 0.0)
+
+        xs = keep.tile([P, S], U8, name="xs", align_bytes=64)
+        nc.vector.tensor_copy(xs[:], xs_all[:].indirect(offs_t[:]))
+
+        w1_grouped = keep.tile([P, PACK * H], BF16, name="w1_grouped", align_bytes=64)
+        dst, src = deal_views(w1_raw, w1_grouped)
+        nc.vector.tensor_copy(out=dst, in_=src)
+        w1_codes = keep.tile([P, H], U32, name="w1_codes", align_bytes=64)
+        w1_scales = keep.tile([P, H], U8, name="w1_scales", align_bytes=64)
+        nc.vector.quantize_mx(out=w1_codes[:].bitcast(FP8X4), scales=w1_scales[:], in_=w1_grouped[:])
+
+        xw = keep.tile([P, S], U32, name="xw", align_bytes=64)
+        nc.vector.tensor_copy(xw[:], xw_all[:].bitcast(U32).indirect(offs_t[:]))
+
+        w2_grouped = keep.tile([P, PACK * N], BF16, name="w2_grouped", align_bytes=64)
+        w2_codes = keep.tile([P, N], U32, name="w2_codes", align_bytes=64)
+        w2_scales = keep.tile([P, N], U8, name="w2_scales", align_bytes=64)
+
+        z_in = [keep.tile([P, BANK, PACK], BF16, name=f"z_in{h}", align_bytes=64) for h in range(2)]
+
+        def pair_views(t, h, lo, hi):
+            src_pair = win[t][:].rearrange("p (e w) -> p w e", e=2)
+            return z_in[h][:, lo:hi, t : t + 2], src_pair[:, h * BANK + lo : h * BANK + hi, :]
+
+        act = {}
+        for t in (1, 3, 0, 2):
+            cols = slice(t * P, (t + 1) * P)
+            y = psum.tile([P, BANK], F32, name="bank")
+            nc.tensor.matmul_mx(
+                out=y[:], lhsT=w1_codes[:, cols].bitcast(FP8X4), lhsT_scale=w1_scales[:, cols],
+                rhs=xw[:].bitcast(FP8X4), rhs_scale=xs[:], start=True, stop=True,
+            )
+            act[t] = keep.tile([P, S], F32, name=f"act{t}")
+            nc.scalar.activation(act[t][:], y[:], GELU)
+
+        for t in (1, 3, 0, 2):
+            nc.vector.tensor_copy(win[t][:].indirect(slot_t[:]), act[t][:])
+            if t % 2:
+                nc.scalar.copy(win[t - 1][:, U : 2 * U], win[t][:])
+            if t == 1:
+                dst, src = deal_views(w2_raw, w2_grouped)
+                nc.scalar.copy(out=dst, in_=src)
+            if t == 3:
+                nc.vector.quantize_mx(out=w2_codes[:].bitcast(FP8X4), scales=w2_scales[:], in_=w2_grouped[:])
+            if t == 0:
+                for h in range(2):
+                    dst, src = pair_views(0, h, 0, BANK)
+                    nc.scalar.copy(out=dst, in_=src)
+
+        dst, src = pair_views(2, 0, 0, BANK)
+        nc.vector.tensor_copy(out=dst, in_=src)
+        dst, src = pair_views(2, 1, 0, BANK // 2)
+        nc.vector.tensor_copy(out=dst, in_=src)
+        dst, src = pair_views(2, 1, BANK // 2, BANK)
+        nc.scalar.copy(out=dst, in_=src)
+
+        z_codes = [keep.tile([P, BANK], U32, name=f"z_codes{h}", align_bytes=64) for h in range(2)]
+        z_scales = [keep.tile([P, BANK], U8, name=f"z_scales{h}", align_bytes=64) for h in range(2)]
+        for h in range(2):
+            nc.vector.quantize_mx(
+                out=z_codes[h][:].bitcast(FP8X4), scales=z_scales[h][:],
+                in_=z_in[h][:].rearrange("p w j -> p (w j)"),
+            )
+
+        out_rows = out.rearrange("(p t) v -> p t v", t=PACK)
+        parts = {}
+        for t in range(PACK + 1):
+            if t < PACK:
+                cols = slice(t * P, (t + 1) * P)
+                hid = keep.tile([P, U], F32, name=f"hid{t}")
+                for h in range(2):
+                    acc = psum.tile([P, BANK], F32, name="bank")
+                    nc.tensor.matmul_mx(
+                        out=acc[:], lhsT=w2_codes[:, cols].bitcast(FP8X4), lhsT_scale=w2_scales[:, cols],
+                        rhs=z_codes[h][:].bitcast(FP8X4), rhs_scale=z_scales[h][:], start=True, stop=True,
+                    )
+                    nc.scalar.copy(hid[:, h * BANK : (h + 1) * BANK], acc[:])
+                first = keep.tile([P, V], F32, name=f"first{t}")
+                second = keep.tile([P, V], F32, name=f"second{t}")
+                nc.vector.tensor_tensor(first[:], hid[:].indirect(c1_t[:]), g1_t[:], MULT)
+            if t > 0:
+                res = keep.tile([P, V], F32, name=f"res{t - 1}")
+                nc.vector.tensor_tensor(res[:], parts[t - 1][0][:], parts[t - 1][1][:], ADD)
+                nc.sync.dma_start(out=out_rows[:, t - 1, :], in_=res[:])
+            if t < PACK:
+                nc.vector.tensor_tensor(second[:], hid[:].indirect(c2_t[:]), g2_t[:], MULT)
+                parts[t] = (first, second)

@@ -21,6 +21,12 @@ PACK = 4
 BANK = 512
 
 
+def combine(nc, keep, out_rows, n, t, toks, first, second):
+    res = keep.tile([P, toks.stop - toks.start], F32, name=f"res{n}")
+    nc.vector.tensor_tensor(res[:], first[:], second[:], ADD)
+    nc.sync.dma_start(out=out_rows[:, t, toks], in_=res[:])
+
+
 def tile_picked_dcomb_gelu_p_kernel(
     tc, x_words, x_scales, w1, w2, g1, g2, offs, slot, c1, c2, out
 ):
@@ -45,6 +51,7 @@ def tile_picked_dcomb_gelu_p_kernel(
                 raw[:].rearrange("p j (m t) -> p m t j", t=PACK),
             )
 
+        w1_raw = load_weight(w1, "w1_raw")
         xs_all = keep.tile([P, T], U8, name="xs_all", align_bytes=64)
         nc.vector.memset(xs_all[:].bitcast(I32), 0)
         offs_t = load_list(offs, "offs_t")
@@ -53,11 +60,11 @@ def tile_picked_dcomb_gelu_p_kernel(
                 out=xs_all[32 * q : 32 * q + 4, :].bitcast(I32),
                 in_=x_scales[0, 4 * q : 4 * q + 4, :].bitcast(I32),
             )
-        w1_raw = load_weight(w1, "w1_raw")
         xw_all = keep.tile([P, T], I32, name="xw_all", align_bytes=64)
         nc.sync.dma_start(out=xw_all[:], in_=x_words[0].rearrange("p c r -> p (c r)").bitcast(I32))
         slot_t = load_list(slot, "slot_t")
-        w2_raw = load_weight(w2, "w2_raw")
+        w2_raw = keep.tile([P, PACK, N], F32, name="w2_raw", tag="w2_raw_then_z", align_bytes=64)
+        nc.sync.dma_start(out=w2_raw[:], in_=w2.rearrange("(p j) c -> p j c", j=PACK))
         c1_t = load_list(c1, "c1_t")
         c2_t = load_list(c2, "c2_t")
         g1_t = keep.tile([P, V], F32, name="g1_t")
@@ -71,89 +78,125 @@ def tile_picked_dcomb_gelu_p_kernel(
             win[t] = keep.tile([P, width], F32, name=f"win{t}")
             nc.vector.memset(win[t][:, 0:U], 0.0)
 
+        w1_grouped, w1_codes, w1_scales = {}, {}, {}
+        for e in (1, 0):
+            w1_grouped[e] = keep.tile([P, 2 * P * PACK], BF16, name=f"w1_grouped{e}", align_bytes=64)
+            w1_codes[e] = keep.tile([P, 2 * P], U32, name=f"w1_codes{e}", align_bytes=64)
+            w1_scales[e] = keep.tile([P, 2 * P], U8, name=f"w1_scales{e}", align_bytes=64)
+            dst = w1_grouped[e][:].rearrange("p (u m j) -> p m u j", u=2, j=PACK)
+            src = w1_raw[:].rearrange("p j (m u e) -> p e m u j", u=2, e=2)[:, e]
+            if e:
+                nc.vector.tensor_copy(out=dst, in_=src)
+            else:
+                nc.scalar.copy(out=dst, in_=src)
+
+        def quantize(codes, scales, grouped):
+            nc.vector.quantize_mx(out=codes.bitcast(FP8X4), scales=scales, in_=grouped)
+
         xs = keep.tile([P, S], U8, name="xs", align_bytes=64)
         nc.vector.tensor_copy(xs[:], xs_all[:].indirect(offs_t[:]))
-
-        w1_grouped = keep.tile([P, PACK * H], BF16, name="w1_grouped", align_bytes=64)
-        dst, src = deal_views(w1_raw, w1_grouped)
-        nc.vector.tensor_copy(out=dst, in_=src)
-        w1_codes = keep.tile([P, H], U32, name="w1_codes", align_bytes=64)
-        w1_scales = keep.tile([P, H], U8, name="w1_scales", align_bytes=64)
-        nc.vector.quantize_mx(out=w1_codes[:].bitcast(FP8X4), scales=w1_scales[:], in_=w1_grouped[:])
+        quantize(w1_codes[1][:], w1_scales[1][:], w1_grouped[1][:])
 
         xw = keep.tile([P, S], U32, name="xw", align_bytes=64)
-        nc.vector.tensor_copy(xw[:], xw_all[:].bitcast(U32).indirect(offs_t[:]))
+        halves = [slice(0, S // 2), slice(S // 2, S)]
+        list_halves = [slice(0, S // 32), slice(S // 32, S // 16)]
+        for h in range(2):
+            nc.vector.tensor_copy(xw[:, halves[h]], xw_all[:].bitcast(U32).indirect(offs_t[:, list_halves[h]]))
+        quantize(w1_codes[0][:], w1_scales[0][:], w1_grouped[0][:])
+
+        def product(lhs_codes, lhs_scales, rhs_codes, rhs_scales, width):
+            bank = psum.tile([P, BANK], F32, name="bank")
+            nc.tensor.matmul_mx(
+                out=bank[:, 0:width], lhsT=lhs_codes.bitcast(FP8X4), lhsT_scale=lhs_scales,
+                rhs=rhs_codes.bitcast(FP8X4), rhs_scale=rhs_scales, start=True, stop=True,
+            )
+            return bank[:, 0:width]
+
+        steps = [(1, halves[0], list_halves[0]), (3, halves[0], list_halves[0]),
+                 (1, halves[1], list_halves[1]), (3, halves[1], list_halves[1]),
+                 (0, slice(0, S), slice(0, S // 16)), (2, slice(0, S), slice(0, S // 16))]
+        acts = []
+        for n, (t, toks, cols) in enumerate(steps):
+            width = toks.stop - toks.start
+            lhs = slice((t // 2) * P, (t // 2 + 1) * P)
+            y = product(w1_codes[t % 2][:, lhs], w1_scales[t % 2][:, lhs], xw[:, toks], xs[:, toks], width)
+            act = keep.tile([P, width], F32, name=f"act{n}")
+            nc.scalar.activation(act[:], y, GELU)
+            acts.append(act)
 
         w2_grouped = keep.tile([P, PACK * N], BF16, name="w2_grouped", align_bytes=64)
-        w2_codes = keep.tile([P, N], U32, name="w2_codes", align_bytes=64)
+        dst, src = deal_views(w2_raw, w2_grouped)
+        nc.scalar.copy(out=dst, in_=src)
+        w2_codes0 = keep.tile([P, P], U32, name="w2_codes0", align_bytes=64)
         w2_scales = keep.tile([P, N], U8, name="w2_scales", align_bytes=64)
 
-        z_in = [keep.tile([P, BANK, PACK], BF16, name=f"z_in{h}", align_bytes=64) for h in range(2)]
+        z_in = keep.tile([P, U * PACK], BF16, name="z_in", tag="w2_raw_then_z", align_bytes=64)
+        Q = U // 4
 
-        def pair_views(t, h, lo, hi):
-            src_pair = win[t][:].rearrange("p (e w) -> p w e", e=2)
-            return z_in[h][:, lo:hi, t : t + 2], src_pair[:, h * BANK + lo : h * BANK + hi, :]
-
-        act = {}
-        for t in (1, 3, 0, 2):
-            cols = slice(t * P, (t + 1) * P)
-            y = psum.tile([P, BANK], F32, name="bank")
-            nc.tensor.matmul_mx(
-                out=y[:], lhsT=w1_codes[:, cols].bitcast(FP8X4), lhsT_scale=w1_scales[:, cols],
-                rhs=xw[:].bitcast(FP8X4), rhs_scale=xs[:], start=True, stop=True,
+        def pair_views(t, q):
+            places = slice(q * Q, (q + 1) * Q)
+            return (
+                z_in[:].rearrange("p (w j) -> p w j", j=PACK)[:, places, t : t + 2],
+                win[t][:].rearrange("p (e w) -> p w e", e=2)[:, places, :],
             )
-            act[t] = keep.tile([P, S], F32, name=f"act{t}")
-            nc.scalar.activation(act[t][:], y[:], GELU)
 
-        for t in (1, 3, 0, 2):
-            nc.vector.tensor_copy(win[t][:].indirect(slot_t[:]), act[t][:])
-            if t % 2:
-                nc.scalar.copy(win[t - 1][:, U : 2 * U], win[t][:])
-            if t == 1:
-                dst, src = deal_views(w2_raw, w2_grouped)
-                nc.scalar.copy(out=dst, in_=src)
-            if t == 3:
-                nc.vector.quantize_mx(out=w2_codes[:].bitcast(FP8X4), scales=w2_scales[:], in_=w2_grouped[:])
-            if t == 0:
-                for h in range(2):
-                    dst, src = pair_views(0, h, 0, BANK)
+        for n, (t, toks, cols) in enumerate(steps):
+            nc.vector.tensor_copy(win[t][:].indirect(slot_t[:, cols]), acts[n][:])
+            if n == 2:
+                nc.scalar.copy(win[0][:, U : 2 * U], win[1][:])
+            if n == 3:
+                nc.sync.dma_start(out=win[2][:, U : 2 * U], in_=win[3][:])
+            if n == 4:
+                quantize(w2_codes0[:], w2_scales[:, 0:P], w2_grouped[:, 0 : PACK * P])
+                for q in range(4):
+                    dst, src = pair_views(0, q)
                     nc.scalar.copy(out=dst, in_=src)
 
-        dst, src = pair_views(2, 0, 0, BANK)
-        nc.vector.tensor_copy(out=dst, in_=src)
-        dst, src = pair_views(2, 1, 0, BANK // 2)
-        nc.vector.tensor_copy(out=dst, in_=src)
-        dst, src = pair_views(2, 1, BANK // 2, BANK)
-        nc.scalar.copy(out=dst, in_=src)
+        z_codes = keep.tile([P, U], U32, name="z_codes", align_bytes=64)
+        z_scales = keep.tile([P, U], U8, name="z_scales", align_bytes=64)
 
-        z_codes = [keep.tile([P, BANK], U32, name=f"z_codes{h}", align_bytes=64) for h in range(2)]
-        z_scales = [keep.tile([P, BANK], U8, name=f"z_scales{h}", align_bytes=64) for h in range(2)]
-        for h in range(2):
-            nc.vector.quantize_mx(
-                out=z_codes[h][:].bitcast(FP8X4), scales=z_scales[h][:],
-                in_=z_in[h][:].rearrange("p w j -> p (w j)"),
-            )
+        def quantize_z(q):
+            quantize(z_codes[:, q * Q : (q + 1) * Q], z_scales[:, q * Q : (q + 1) * Q],
+                     z_in[:, q * Q * PACK : (q + 1) * Q * PACK])
+
+        dst, src = pair_views(2, 3)
+        nc.scalar.copy(out=dst, in_=src)
+        for q in range(3):
+            dst, src = pair_views(2, q)
+            nc.vector.tensor_copy(out=dst, in_=src)
+            if q > 0:
+                quantize_z(q - 1)
+        quantize_z(2)
+        quantize_z(3)
+
+        w2_codes_rest = keep.tile([P, N - P], U32, name="w2_codes_rest", tag="w2_raw_then_z", align_bytes=64)
+        quantize(w2_codes_rest[:, 0:P], w2_scales[:, P : 2 * P], w2_grouped[:, PACK * P : 2 * PACK * P])
+        quantize(w2_codes_rest[:, P : 3 * P], w2_scales[:, 2 * P : N], w2_grouped[:, 2 * PACK * P : PACK * N])
 
         out_rows = out.rearrange("(p t) v -> p t v", t=PACK)
-        parts = {}
-        for t in range(PACK + 1):
-            if t < PACK:
-                cols = slice(t * P, (t + 1) * P)
-                hid = keep.tile([P, U], F32, name=f"hid{t}")
-                for h in range(2):
-                    acc = psum.tile([P, BANK], F32, name="bank")
-                    nc.tensor.matmul_mx(
-                        out=acc[:], lhsT=w2_codes[:, cols].bitcast(FP8X4), lhsT_scale=w2_scales[:, cols],
-                        rhs=z_codes[h][:].bitcast(FP8X4), rhs_scale=z_scales[h][:], start=True, stop=True,
-                    )
-                    nc.scalar.copy(hid[:, h * BANK : (h + 1) * BANK], acc[:])
-                first = keep.tile([P, V], F32, name=f"first{t}")
-                second = keep.tile([P, V], F32, name=f"second{t}")
-                nc.vector.tensor_tensor(first[:], hid[:].indirect(c1_t[:]), g1_t[:], MULT)
-            if t > 0:
-                res = keep.tile([P, V], F32, name=f"res{t - 1}")
-                nc.vector.tensor_tensor(res[:], parts[t - 1][0][:], parts[t - 1][1][:], ADD)
-                nc.sync.dma_start(out=out_rows[:, t - 1, :], in_=res[:])
-            if t < PACK:
-                nc.vector.tensor_tensor(second[:], hid[:].indirect(c2_t[:]), g2_t[:], MULT)
-                parts[t] = (first, second)
+        hid = []
+        for t in range(PACK):
+            hid.append(keep.tile([P, U], F32, name=f"hid{t}"))
+            lhs_codes = w2_codes0[:] if t == 0 else w2_codes_rest[:, (t - 1) * P : t * P]
+            width = Q if t == 0 else BANK
+            for lo in range(0, U, width):
+                places = slice(lo, lo + width)
+                acc = product(lhs_codes, w2_scales[:, t * P : (t + 1) * P], z_codes[:, places], z_scales[:, places], width)
+                if t == 0 and lo + width == U:
+                    nc.vector.tensor_copy(hid[t][:, places], acc)
+                else:
+                    nc.scalar.copy(hid[t][:, places], acc)
+
+        pieces = [(t, slice(0, V), slice(0, V // 16)) for t in range(PACK - 1)]
+        pieces = pieces + [(PACK - 1, halves[h], list_halves[h]) for h in range(2)]
+        pending = None
+        for n, (t, toks, cols) in enumerate(pieces):
+            width = toks.stop - toks.start
+            first = keep.tile([P, width], F32, name=f"first{n}")
+            second = keep.tile([P, width], F32, name=f"second{n}")
+            nc.vector.tensor_tensor(first[:], hid[t][:].indirect(c1_t[:, cols]), g1_t[:, toks], MULT)
+            if pending is not None:
+                combine(nc, keep, out_rows, *pending)
+            nc.vector.tensor_tensor(second[:], hid[t][:].indirect(c2_t[:, cols]), g2_t[:, toks], MULT)
+            pending = (n, t, toks, first, second)
+        combine(nc, keep, out_rows, *pending)

@@ -1,6 +1,7 @@
 from contextlib import ExitStack
 
 import concourse.mybir as mybir
+from concourse.masks import make_identity
 
 K, T, S, V, N, U, H = 512, 2048, 512, 512, 512, 1024, 512
 FLOPS = 2 * K * H * S + 2 * H * N * U
@@ -21,19 +22,13 @@ PACK = 4
 BANK = 512
 
 
-def combine(nc, keep, out_rows, n, t, toks, first, second):
-    res = keep.tile([P, toks.stop - toks.start], F32, name=f"res{n}")
-    nc.vector.tensor_tensor(res[:], first[:], second[:], ADD)
-    nc.sync.dma_start(out=out_rows[:, t, toks], in_=res[:])
-
-
 def tile_picked_dcomb_gelu_p_kernel(
     tc, x_words, x_scales, w1, w2, g1, g2, offs, slot, c1, c2, out
 ):
     nc = tc.nc
     with ExitStack() as ctx:
         keep = ctx.enter_context(tc.tile_pool(name="keep", bufs=1))
-        psum = ctx.enter_context(tc.psum_pool(name="psum", bufs=8))
+        psum = ctx.enter_context(tc.psum_pool(name="psum", bufs=1))
 
         def load_list(src, name):
             tile = keep.tile([P, S // 16], U16, name=name)
@@ -51,15 +46,15 @@ def tile_picked_dcomb_gelu_p_kernel(
                 raw[:].rearrange("p j (m t) -> p m t j", t=PACK),
             )
 
-        w1_raw = load_weight(w1, "w1_raw")
+        w1_raw = keep.tile([P, PACK, H], F32, name="w1_raw")
+        w1_rows = w1.rearrange("(p j) c -> p j c", j=PACK)
+        nc.sync.dma_start(out=w1_raw[:, 0:2, :], in_=w1_rows[:, 0:2, :])
         xs_all = keep.tile([P, T], U8, name="xs_all", align_bytes=64)
         nc.vector.memset(xs_all[:].bitcast(I32), 0)
         offs_t = load_list(offs, "offs_t")
-        for q in range(4):
-            nc.sync.dma_start(
-                out=xs_all[32 * q : 32 * q + 4, :].bitcast(I32),
-                in_=x_scales[0, 4 * q : 4 * q + 4, :].bitcast(I32),
-            )
+        for r in range(4):
+            nc.sync.dma_start(out=xs_all[r:P:32, :].bitcast(I32), in_=x_scales[0, r:16:4, :].bitcast(I32))
+        nc.sync.dma_start(out=w1_raw[:, 2:4, :], in_=w1_rows[:, 2:4, :])
         xw_all = keep.tile([P, T], I32, name="xw_all", align_bytes=64)
         nc.sync.dma_start(out=xw_all[:], in_=x_words[0].rearrange("p c r -> p (c r)").bitcast(I32))
         slot_t = load_list(slot, "slot_t")
@@ -76,7 +71,13 @@ def tile_picked_dcomb_gelu_p_kernel(
         for t in (1, 3, 0, 2):
             width = U if t % 2 else 2 * U
             win[t] = keep.tile([P, width], F32, name=f"win{t}")
-            nc.vector.memset(win[t][:, 0:U], 0.0)
+            if t % 2:
+                nc.vector.memset(win[t][:], 0.0)
+            else:
+                nc.scalar.copy(win[t][:, 0:U], win[t + 1][:])
+
+        xs = keep.tile([P, S], U8, name="xs", align_bytes=64)
+        nc.vector.tensor_copy(xs[:], xs_all[:].indirect(offs_t[:]))
 
         w1_grouped, w1_codes, w1_scales = {}, {}, {}
         for e in (1, 0):
@@ -93,8 +94,6 @@ def tile_picked_dcomb_gelu_p_kernel(
         def quantize(codes, scales, grouped):
             nc.vector.quantize_mx(out=codes.bitcast(FP8X4), scales=scales, in_=grouped)
 
-        xs = keep.tile([P, S], U8, name="xs", align_bytes=64)
-        nc.vector.tensor_copy(xs[:], xs_all[:].indirect(offs_t[:]))
         quantize(w1_codes[1][:], w1_scales[1][:], w1_grouped[1][:])
 
         xw = keep.tile([P, S], U32, name="xw", align_bytes=64)
@@ -104,25 +103,21 @@ def tile_picked_dcomb_gelu_p_kernel(
             nc.vector.tensor_copy(xw[:, halves[h]], xw_all[:].bitcast(U32).indirect(offs_t[:, list_halves[h]]))
         quantize(w1_codes[0][:], w1_scales[0][:], w1_grouped[0][:])
 
-        def product(lhs_codes, lhs_scales, rhs_codes, rhs_scales, width):
-            bank = psum.tile([P, BANK], F32, name="bank")
+        def product(lhs_codes, lhs_scales, rhs_codes, rhs_scales, width, b):
+            bank = psum.tile([P, BANK], F32, name=f"bank{b}")
             nc.tensor.matmul_mx(
                 out=bank[:, 0:width], lhsT=lhs_codes.bitcast(FP8X4), lhsT_scale=lhs_scales,
                 rhs=rhs_codes.bitcast(FP8X4), rhs_scale=rhs_scales, start=True, stop=True,
             )
             return bank[:, 0:width]
 
-        steps = [(1, halves[0], list_halves[0]), (3, halves[0], list_halves[0]),
-                 (1, halves[1], list_halves[1]), (3, halves[1], list_halves[1]),
-                 (0, slice(0, S), slice(0, S // 16)), (2, slice(0, S), slice(0, S // 16))]
-        acts = []
-        for n, (t, toks, cols) in enumerate(steps):
-            width = toks.stop - toks.start
+        act = {t: keep.tile([P, S], F32, name=f"act{t}") for t in range(PACK)}
+        products = [(1, 0, 128), (3, 0, 128), (1, 128, 256), (1, 256, 512), (3, 128, 256), (3, 256, 512), (0, 0, 512), (2, 0, 512)]
+        for n, (t, lo, hi) in enumerate(products):
             lhs = slice((t // 2) * P, (t // 2 + 1) * P)
-            y = product(w1_codes[t % 2][:, lhs], w1_scales[t % 2][:, lhs], xw[:, toks], xs[:, toks], width)
-            act = keep.tile([P, width], F32, name=f"act{n}")
-            nc.scalar.activation(act[:], y, GELU)
-            acts.append(act)
+            y = product(w1_codes[t % 2][:, lhs], w1_scales[t % 2][:, lhs], xw[:, lo:hi], xs[:, lo:hi], hi - lo, n)
+            nc.scalar.activation(act[t][:, lo:hi], y, GELU)
+        steps = [(1, 0, 128), (3, 0, 128), (1, 128, 512), (3, 128, 512), (0, 0, 512), (2, 0, 512)]
 
         w2_grouped = keep.tile([P, PACK * N], BF16, name="w2_grouped", align_bytes=64)
         dst, src = deal_views(w2_raw, w2_grouped)
@@ -133,15 +128,15 @@ def tile_picked_dcomb_gelu_p_kernel(
         z_in = keep.tile([P, U * PACK], BF16, name="z_in", tag="w2_raw_then_z", align_bytes=64)
         Q = U // 4
 
-        def pair_views(t, q):
-            places = slice(q * Q, (q + 1) * Q)
+        def pair_views(t, lo, hi):
+            places = slice(lo, hi)
             return (
                 z_in[:].rearrange("p (w j) -> p w j", j=PACK)[:, places, t : t + 2],
                 win[t][:].rearrange("p (e w) -> p w e", e=2)[:, places, :],
             )
 
-        for n, (t, toks, cols) in enumerate(steps):
-            nc.vector.tensor_copy(win[t][:].indirect(slot_t[:, cols]), acts[n][:])
+        for n, (t, lo, hi) in enumerate(steps):
+            nc.vector.tensor_copy(win[t][:].indirect(slot_t[:, lo // 16 : hi // 16]), act[t][:, lo:hi])
             if n == 2:
                 nc.scalar.copy(win[0][:, U : 2 * U], win[1][:])
             if n == 3:
@@ -149,7 +144,7 @@ def tile_picked_dcomb_gelu_p_kernel(
             if n == 4:
                 quantize(w2_codes0[:], w2_scales[:, 0:P], w2_grouped[:, 0 : PACK * P])
                 for q in range(4):
-                    dst, src = pair_views(0, q)
+                    dst, src = pair_views(0, q * Q, (q + 1) * Q)
                     nc.scalar.copy(out=dst, in_=src)
 
         z_codes = keep.tile([P, U], U32, name="z_codes", align_bytes=64)
@@ -159,10 +154,11 @@ def tile_picked_dcomb_gelu_p_kernel(
             quantize(z_codes[:, q * Q : (q + 1) * Q], z_scales[:, q * Q : (q + 1) * Q],
                      z_in[:, q * Q * PACK : (q + 1) * Q * PACK])
 
-        dst, src = pair_views(2, 3)
-        nc.scalar.copy(out=dst, in_=src)
-        for q in range(3):
-            dst, src = pair_views(2, q)
+        for lo, hi in ((640, 768), (768, U)):
+            dst, src = pair_views(2, lo, hi)
+            nc.scalar.copy(out=dst, in_=src)
+        for q, (lo, hi) in enumerate(((0, 256), (256, 512), (512, 640))):
+            dst, src = pair_views(2, lo, hi)
             nc.vector.tensor_copy(out=dst, in_=src)
             if q > 0:
                 quantize_z(q - 1)
@@ -175,28 +171,55 @@ def tile_picked_dcomb_gelu_p_kernel(
 
         out_rows = out.rearrange("(p t) v -> p t v", t=PACK)
         hid = []
+        hid_banks = [(0, 1, 2, 3), (4, 5), (6, 7), (0, 1)]
         for t in range(PACK):
             hid.append(keep.tile([P, U], F32, name=f"hid{t}"))
             lhs_codes = w2_codes0[:] if t == 0 else w2_codes_rest[:, (t - 1) * P : t * P]
             width = Q if t == 0 else BANK
             for lo in range(0, U, width):
                 places = slice(lo, lo + width)
-                acc = product(lhs_codes, w2_scales[:, t * P : (t + 1) * P], z_codes[:, places], z_scales[:, places], width)
-                if t == 0 and lo + width == U:
-                    nc.vector.tensor_copy(hid[t][:, places], acc)
-                else:
-                    nc.scalar.copy(hid[t][:, places], acc)
+                acc = product(lhs_codes, w2_scales[:, t * P : (t + 1) * P], z_codes[:, places], z_scales[:, places], width, hid_banks[t][lo // width])
+                nc.scalar.copy(hid[t][:, places], acc)
 
-        pieces = [(t, slice(0, V), slice(0, V // 16)) for t in range(PACK - 1)]
-        pieces = pieces + [(PACK - 1, halves[h], list_halves[h]) for h in range(2)]
-        pending = None
-        for n, (t, toks, cols) in enumerate(pieces):
-            width = toks.stop - toks.start
-            first = keep.tile([P, width], F32, name=f"first{n}")
-            second = keep.tile([P, width], F32, name=f"second{n}")
-            nc.vector.tensor_tensor(first[:], hid[t][:].indirect(c1_t[:, cols]), g1_t[:, toks], MULT)
-            if pending is not None:
-                combine(nc, keep, out_rows, *pending)
-            nc.vector.tensor_tensor(second[:], hid[t][:].indirect(c2_t[:, cols]), g2_t[:, toks], MULT)
-            pending = (n, t, toks, first, second)
-        combine(nc, keep, out_rows, *pending)
+        ident = keep.tile([P, P], F32, name="ident")
+        make_identity(nc, ident[:])
+        first = [keep.tile([P, V], F32, name=f"first{t}") for t in range(PACK)]
+        second = [keep.tile([P, V], F32, name=f"second{t}") for t in range(PACK)]
+
+        def look_up(dst, t, list_t, g_t, lo, hi):
+            nc.vector.tensor_tensor(dst[:, lo:hi], hid[t][:].indirect(list_t[:, lo // 16 : hi // 16]), g_t[:, lo:hi], MULT)
+
+        def add_on_vector(t, lo, hi):
+            res = keep.tile([P, hi - lo], F32, name=f"res{t}_{lo}")
+            nc.vector.tensor_tensor(res[:], first[t][:, lo:hi], second[t][:, lo:hi], ADD)
+            nc.sync.dma_start(out=out_rows[:, t, lo:hi], in_=res[:])
+
+        def add_on_tensor(t):
+            turned = psum.tile([P, BANK], F32, name=f"bank{2 + t}")
+            for b in range(V // P):
+                cols = slice(b * P, (b + 1) * P)
+                nc.tensor.matmul(turned[:, cols], lhsT=first[t][:, cols], rhs=ident[:], is_transpose=True, start=True, stop=False)
+                nc.tensor.matmul(turned[:, cols], lhsT=second[t][:, cols], rhs=ident[:], is_transpose=True, start=False, stop=True)
+            total = keep.tile([P, V], F32, name=f"total{t}")
+            nc.scalar.copy(total[:], turned[:])
+            back = psum.tile([P, BANK], F32, name=f"bank{4 + t}")
+            for b in range(V // P):
+                cols = slice(b * P, (b + 1) * P)
+                nc.tensor.transpose(back[:, cols], total[:, cols], ident[:])
+            res = keep.tile([P, V], F32, name=f"res{t}")
+            nc.scalar.copy(res[:], back[:])
+            nc.scalar.dma_start(out=out_rows[:, t, :], in_=res[:])
+
+        for t in range(2):
+            look_up(first[t], t, c1_t, g1_t, 0, V)
+            look_up(second[t], t, c2_t, g2_t, 0, V)
+            add_on_tensor(t)
+        last = PACK - 1
+        look_up(first[2], 2, c1_t, g1_t, 0, V)
+        look_up(second[2], 2, c2_t, g2_t, 0, V)
+        look_up(first[last], last, c1_t, g1_t, 0, V)
+        add_on_vector(2, 0, V)
+        look_up(second[last], last, c2_t, g2_t, 0, 384)
+        look_up(second[last], last, c2_t, g2_t, 384, V)
+        add_on_vector(last, 0, 384)
+        add_on_vector(last, 384, V)

from contextlib import ExitStack

import concourse.mybir as mybir
from concourse.masks import make_identity

K, T, S, V, N, U, H = 512, 2048, 512, 512, 512, 1024, 512
FLOPS = 2 * K * H * S + 2 * H * N * U

F32 = mybir.dt.float32
BF16 = mybir.dt.bfloat16
I32 = mybir.dt.int32
U32 = mybir.dt.uint32
U16 = mybir.dt.uint16
U8 = mybir.dt.uint8
FP8X4 = mybir.dt.float8_e4m3fn_x4
MULT = mybir.AluOpType.mult
ADD = mybir.AluOpType.add
GELU = mybir.ActivationFunctionType.Gelu_apprx_tanh

P = 128
PACK = 4
BANK = 512


def tile_picked_dcomb_gelu_p_kernel(
    tc, x_words, x_scales, w1, w2, g1, g2, offs, slot, c1, c2, out
):
    nc = tc.nc
    with ExitStack() as ctx:
        keep = ctx.enter_context(tc.tile_pool(name="keep", bufs=1))
        psum = ctx.enter_context(tc.psum_pool(name="psum", bufs=1))

        def load_list(src, name):
            tile = keep.tile([P, S // 16], U16, name=name)
            nc.sync.dma_start(tile[:], src)
            return tile

        def load_weight(src, name):
            raw = keep.tile([P, PACK, BANK], F32, name=name)
            nc.sync.dma_start(out=raw[:], in_=src.rearrange("(p j) c -> p j c", j=PACK))
            return raw

        def deal_views(raw, grouped):
            return (
                grouped[:].rearrange("p (t m j) -> p m t j", t=PACK, j=PACK),
                raw[:].rearrange("p j (m t) -> p m t j", t=PACK),
            )

        w1_raw = keep.tile([P, PACK, H], F32, name="w1_raw")
        w1_rows = w1.rearrange("(p j) c -> p j c", j=PACK)
        nc.sync.dma_start(out=w1_raw[:, 0:2, :], in_=w1_rows[:, 0:2, :])
        xs_all = keep.tile([P, T], U8, name="xs_all", align_bytes=64)
        nc.vector.memset(xs_all[:].bitcast(I32), 0)
        offs_t = load_list(offs, "offs_t")
        for r in range(4):
            nc.sync.dma_start(out=xs_all[r:P:32, :].bitcast(I32), in_=x_scales[0, r:16:4, :].bitcast(I32))
        nc.sync.dma_start(out=w1_raw[:, 2:4, :], in_=w1_rows[:, 2:4, :])
        xw_all = keep.tile([P, T], I32, name="xw_all", align_bytes=64)
        nc.sync.dma_start(out=xw_all[:], in_=x_words[0].rearrange("p c r -> p (c r)").bitcast(I32))
        slot_t = load_list(slot, "slot_t")
        w2_raw = keep.tile([P, PACK, N], F32, name="w2_raw", tag="w2_raw_then_z", align_bytes=64)
        nc.sync.dma_start(out=w2_raw[:], in_=w2.rearrange("(p j) c -> p j c", j=PACK))
        c1_t = load_list(c1, "c1_t")
        c2_t = load_list(c2, "c2_t")
        g1_t = keep.tile([P, V], F32, name="g1_t")
        nc.sync.dma_start(out=g1_t[:], in_=g1)
        g2_t = keep.tile([P, V], F32, name="g2_t")
        nc.sync.dma_start(out=g2_t[:], in_=g2)

        win = {}
        for t in (1, 3, 0, 2):
            width = U if t % 2 else 2 * U
            win[t] = keep.tile([P, width], F32, name=f"win{t}")
            if t % 2:
                nc.vector.memset(win[t][:], 0.0)
            else:
                nc.scalar.copy(win[t][:, 0:U], win[t + 1][:])

        xs = keep.tile([P, S], U8, name="xs", align_bytes=64)
        nc.vector.tensor_copy(xs[:], xs_all[:].indirect(offs_t[:]))

        w1_grouped, w1_codes, w1_scales = {}, {}, {}
        for e in (1, 0):
            w1_grouped[e] = keep.tile([P, 2 * P * PACK], BF16, name=f"w1_grouped{e}", align_bytes=64)
            w1_codes[e] = keep.tile([P, 2 * P], U32, name=f"w1_codes{e}", align_bytes=64)
            w1_scales[e] = keep.tile([P, 2 * P], U8, name=f"w1_scales{e}", align_bytes=64)
            dst = w1_grouped[e][:].rearrange("p (u m j) -> p m u j", u=2, j=PACK)
            src = w1_raw[:].rearrange("p j (m u e) -> p e m u j", u=2, e=2)[:, e]
            if e:
                nc.vector.tensor_copy(out=dst, in_=src)
            else:
                nc.scalar.copy(out=dst, in_=src)

        def quantize(codes, scales, grouped):
            nc.vector.quantize_mx(out=codes.bitcast(FP8X4), scales=scales, in_=grouped)

        quantize(w1_codes[1][:], w1_scales[1][:], w1_grouped[1][:])

        xw = keep.tile([P, S], U32, name="xw", align_bytes=64)
        halves = [slice(0, S // 2), slice(S // 2, S)]
        list_halves = [slice(0, S // 32), slice(S // 32, S // 16)]
        for h in range(2):
            nc.vector.tensor_copy(xw[:, halves[h]], xw_all[:].bitcast(U32).indirect(offs_t[:, list_halves[h]]))
        quantize(w1_codes[0][:], w1_scales[0][:], w1_grouped[0][:])

        def product(lhs_codes, lhs_scales, rhs_codes, rhs_scales, width, b):
            bank = psum.tile([P, BANK], F32, name=f"bank{b}")
            nc.tensor.matmul_mx(
                out=bank[:, 0:width], lhsT=lhs_codes.bitcast(FP8X4), lhsT_scale=lhs_scales,
                rhs=rhs_codes.bitcast(FP8X4), rhs_scale=rhs_scales, start=True, stop=True,
            )
            return bank[:, 0:width]

        act = {t: keep.tile([P, S], F32, name=f"act{t}") for t in range(PACK)}
        products = [(1, 0, 128), (3, 0, 128), (1, 128, 256), (1, 256, 512), (3, 128, 256), (3, 256, 512), (0, 0, 512), (2, 0, 512)]
        for n, (t, lo, hi) in enumerate(products):
            lhs = slice((t // 2) * P, (t // 2 + 1) * P)
            y = product(w1_codes[t % 2][:, lhs], w1_scales[t % 2][:, lhs], xw[:, lo:hi], xs[:, lo:hi], hi - lo, n)
            nc.scalar.activation(act[t][:, lo:hi], y, GELU)
        steps = [(1, 0, 128), (3, 0, 128), (1, 128, 512), (3, 128, 512), (0, 0, 512), (2, 0, 512)]

        w2_grouped = keep.tile([P, PACK * N], BF16, name="w2_grouped", align_bytes=64)
        dst, src = deal_views(w2_raw, w2_grouped)
        nc.scalar.copy(out=dst, in_=src)
        w2_codes0 = keep.tile([P, P], U32, name="w2_codes0", align_bytes=64)
        w2_scales = keep.tile([P, N], U8, name="w2_scales", align_bytes=64)

        z_in = keep.tile([P, U * PACK], BF16, name="z_in", tag="w2_raw_then_z", align_bytes=64)
        Q = U // 4

        def pair_views(t, lo, hi):
            places = slice(lo, hi)
            return (
                z_in[:].rearrange("p (w j) -> p w j", j=PACK)[:, places, t : t + 2],
                win[t][:].rearrange("p (e w) -> p w e", e=2)[:, places, :],
            )

        for n, (t, lo, hi) in enumerate(steps):
            nc.vector.tensor_copy(win[t][:].indirect(slot_t[:, lo // 16 : hi // 16]), act[t][:, lo:hi])
            if n == 2:
                nc.scalar.copy(win[0][:, U : 2 * U], win[1][:])
            if n == 3:
                nc.sync.dma_start(out=win[2][:, U : 2 * U], in_=win[3][:])
            if n == 4:
                quantize(w2_codes0[:], w2_scales[:, 0:P], w2_grouped[:, 0 : PACK * P])
                for q in range(4):
                    dst, src = pair_views(0, q * Q, (q + 1) * Q)
                    nc.scalar.copy(out=dst, in_=src)

        z_codes = keep.tile([P, U], U32, name="z_codes", align_bytes=64)
        z_scales = keep.tile([P, U], U8, name="z_scales", align_bytes=64)

        def quantize_z(q):
            quantize(z_codes[:, q * Q : (q + 1) * Q], z_scales[:, q * Q : (q + 1) * Q],
                     z_in[:, q * Q * PACK : (q + 1) * Q * PACK])

        for lo, hi in ((640, 768), (768, U)):
            dst, src = pair_views(2, lo, hi)
            nc.scalar.copy(out=dst, in_=src)
        for q, (lo, hi) in enumerate(((0, 256), (256, 512), (512, 640))):
            dst, src = pair_views(2, lo, hi)
            nc.vector.tensor_copy(out=dst, in_=src)
            if q > 0:
                quantize_z(q - 1)
        quantize_z(2)
        quantize_z(3)

        w2_codes_rest = keep.tile([P, N - P], U32, name="w2_codes_rest", tag="w2_raw_then_z", align_bytes=64)
        quantize(w2_codes_rest[:, 0:P], w2_scales[:, P : 2 * P], w2_grouped[:, PACK * P : 2 * PACK * P])
        quantize(w2_codes_rest[:, P : 3 * P], w2_scales[:, 2 * P : N], w2_grouped[:, 2 * PACK * P : PACK * N])

        out_rows = out.rearrange("(p t) v -> p t v", t=PACK)
        hid = []
        hid_banks = [(0, 1, 2, 3), (4, 5), (6, 7), (0, 1)]
        for t in range(PACK):
            hid.append(keep.tile([P, U], F32, name=f"hid{t}"))
            lhs_codes = w2_codes0[:] if t == 0 else w2_codes_rest[:, (t - 1) * P : t * P]
            width = Q if t == 0 else BANK
            for lo in range(0, U, width):
                places = slice(lo, lo + width)
                acc = product(lhs_codes, w2_scales[:, t * P : (t + 1) * P], z_codes[:, places], z_scales[:, places], width, hid_banks[t][lo // width])
                nc.scalar.copy(hid[t][:, places], acc)

        ident = keep.tile([P, P], F32, name="ident")
        make_identity(nc, ident[:])
        first = [keep.tile([P, V], F32, name=f"first{t}") for t in range(PACK)]
        second = [keep.tile([P, V], F32, name=f"second{t}") for t in range(PACK)]

        def look_up(dst, t, list_t, g_t, lo, hi):
            nc.vector.tensor_tensor(dst[:, lo:hi], hid[t][:].indirect(list_t[:, lo // 16 : hi // 16]), g_t[:, lo:hi], MULT)

        def add_on_vector(t, lo, hi):
            res = keep.tile([P, hi - lo], F32, name=f"res{t}_{lo}")
            nc.vector.tensor_tensor(res[:], first[t][:, lo:hi], second[t][:, lo:hi], ADD)
            nc.sync.dma_start(out=out_rows[:, t, lo:hi], in_=res[:])

        def add_on_tensor(t):
            turned = psum.tile([P, BANK], F32, name=f"bank{2 + t}")
            for b in range(V // P):
                cols = slice(b * P, (b + 1) * P)
                nc.tensor.matmul(turned[:, cols], lhsT=first[t][:, cols], rhs=ident[:], is_transpose=True, start=True, stop=False)
                nc.tensor.matmul(turned[:, cols], lhsT=second[t][:, cols], rhs=ident[:], is_transpose=True, start=False, stop=True)
            total = keep.tile([P, V], F32, name=f"total{t}")
            nc.scalar.copy(total[:], turned[:])
            back = psum.tile([P, BANK], F32, name=f"bank{4 + t}")
            for b in range(V // P):
                cols = slice(b * P, (b + 1) * P)
                nc.tensor.transpose(back[:, cols], total[:, cols], ident[:])
            res = keep.tile([P, V], F32, name=f"res{t}")
            nc.scalar.copy(res[:], back[:])
            nc.scalar.dma_start(out=out_rows[:, t, :], in_=res[:])

        for t in range(2):
            look_up(first[t], t, c1_t, g1_t, 0, V)
            look_up(second[t], t, c2_t, g2_t, 0, V)
            add_on_tensor(t)
        last = PACK - 1
        look_up(first[2], 2, c1_t, g1_t, 0, V)
        look_up(second[2], 2, c2_t, g2_t, 0, V)
        look_up(first[last], last, c1_t, g1_t, 0, V)
        add_on_vector(2, 0, V)
        look_up(second[last], last, c2_t, g2_t, 0, 384)
        look_up(second[last], last, c2_t, g2_t, 384, V)
        add_on_vector(last, 0, 384)
        add_on_vector(last, 384, V)
